import numpy as np
import ml_dtypes


def mxq(x, axis, fmt="e4m3"):
    dtype, down = {"e4m3": (ml_dtypes.float8_e4m3fn, 7), "e5m2": (ml_dtypes.float8_e5m2, 14)}[fmt]
    v = np.moveaxis(np.asarray(x, np.float32).astype(ml_dtypes.bfloat16).astype(np.float64), axis, -1)
    blocks = v.reshape(v.shape[:-1] + (-1, 32))
    amax = np.abs(blocks).max(-1, keepdims=True)
    byte = np.maximum(np.where(amax > 0, np.frexp(amax)[1] - 1 + 127, 0) - down, 1)
    scale = np.exp2(byte - 127.0)
    codes = (blocks / scale).astype(np.float32).astype(dtype).astype(np.float64)
    return np.moveaxis((codes * scale).reshape(v.shape), -1, axis)


WIDE = False


def mx_kscale(k):
    if not WIDE:
        return np.ones(k)
    levels = np.array([10, -10, 5, -5, 0])
    if k % 512:
        return np.exp2(np.random.permutation(np.resize(levels, k // 32))).repeat(32)
    a = np.empty((k // 512, 16))
    for p in range(k // 512):
        a[p, :8] = np.random.permutation(np.resize(levels, 8))
        for g in range(8):
            far = levels[np.abs(levels - a[p, g]) >= 10]
            a[p, g + 8] = far[np.random.randint(len(far))]
    return np.exp2(a.ravel()).repeat(32)


def f64(x):
    return np.asarray(x).astype(np.float64)


def striped(idx):
    return np.tile(idx.reshape(-1, 16).T, (8, 1)).astype(np.uint16)


def unstriped(offs):
    return offs[:16].T.reshape(-1).astype(np.int64)


E2M1 = np.array([0.0, 0.5, 1.0, 1.5, 2.0, 3.0, 4.0, 6.0, -0.0, -0.5, -1.0, -1.5, -2.0, -3.0, -4.0, -6.0])


def pack_weight(w, fmt):
    k, n = w.shape
    w = f64(np.asarray(w, np.float32).astype(ml_dtypes.bfloat16)).reshape(k // 32, 32, n)
    amax = np.abs(w).max(1)
    if fmt == "e4m3":
        byte = np.frexp(amax)[1] - 1 + 127 - 7
    else:
        mant, ex = np.frexp(amax / 6.0)
        byte = np.where(mant > 0.5, ex, ex - 1) + 127
    byte = np.clip(np.where(amax > 0, byte, 1), 1, 254)
    scaled = (w * np.exp2(127.0 - byte)[:, None, :]).reshape(k, n).astype(np.float32)
    by_word = np.ascontiguousarray(scaled.reshape(k // 512, 128, 4, n).transpose(0, 1, 3, 2))
    if fmt == "e4m3":
        words = by_word.astype(ml_dtypes.float8_e4m3fn).view(np.uint8)
    else:
        c = by_word.astype(ml_dtypes.float4_e2m1fn).view(np.uint8) & 0xF
        words = (c[..., 0::2] | (c[..., 1::2] << 4)).reshape(k // 512, 128, 2 * n)
    return np.ascontiguousarray(words), np.ascontiguousarray(byte.astype(np.uint8).reshape(k // 512, 16, n))


def unpack_weight(words, scales, fmt):
    g, _, n = scales.shape
    words = np.ascontiguousarray(words).reshape(g, 128, n, -1)
    if fmt == "e4m3":
        vals = words.view(ml_dtypes.float8_e4m3fn).astype(np.float64)
    else:
        nib = np.empty((g, 128, n, 4), np.uint8)
        nib[..., 0::2] = words & 0xF
        nib[..., 1::2] = words >> 4
        vals = E2M1[nib]
    vals = vals * np.repeat(np.exp2(scales.astype(np.float64) - 127.0), 8, axis=1)[..., None]
    return vals.transpose(0, 1, 3, 2).reshape(g * 512, n)


def gelu(v):
    return 0.5 * v * (1.0 + np.tanh(np.sqrt(2.0 / np.pi) * (v + 0.044715 * v**3)))


K, H, T, S, T2, P = 1024, 512, 4096, 1024, 2048, 1024

def setup_inputs():
    n = np.random.standard_normal
    s = mx_kscale(K)[:, None]
    u = mx_kscale(H)[:, None]
    tab_words, tab_scales = pack_weight(n((K, T)) * s, "e4m3")
    w2_words, w2_scales = pack_weight(n((H, H)) / np.sqrt(H) / u * u.T, "e2m1")
    return {
        "tab_words": tab_words, "tab_scales": tab_scales,
        "offs": striped(np.random.permutation(T)[:S]),
        "offs2": striped(np.random.permutation(T2)[:S]),
        "offs3": striped(np.random.permutation(T2)[:P]),
        "offs4": striped(np.random.permutation(T2)[:P]),
        "w1": (n((K, H)) / np.sqrt(K) / s * u.T).astype(np.float32),
        "lim": (n((H, S)) * u).astype(np.float32),
        "page0": (n((H, T2)) * u).astype(np.float32),
        "wgs": np.exp(0.3 * n((128, S))).astype(np.float32),
        "bias": (0.7 * n(H) * u[:, 0]).astype(np.float32),
        "w2_words": w2_words, "w2_scales": w2_scales,
        "w3": (n((K, H)) / np.sqrt(K) / s * u.T).astype(np.float32),
        "gain": np.exp(0.4 * n(H)).astype(np.float32),
        "wgo": np.exp(0.3 * n((128, P))).astype(np.float32),
    }

def reference(tab_words, tab_scales, offs, offs2, offs3, offs4, w1, lim, page0, wgs, bias, w2_words, w2_scales, w3, gain, wgo):
    v = unpack_weight(tab_words, tab_scales, "e4m3")[:, unstriped(offs)]
    h = np.minimum(mxq(f64(w1), 0, "e4m3").T @ v, f64(lim))
    page = f64(page0).copy()
    page[:, unstriped(offs2)] = np.tile(f64(wgs), (H // 128, 1)) * h
    x = page[:, unstriped(offs3)] + f64(bias)[:, None]
    w2 = unpack_weight(w2_words, w2_scales, "e2m1")
    y = w2.T @ mxq(x, 0, "e4m3") + mxq(f64(w3), 0, "e4m3").T @ v
    y = np.abs(y) * f64(gain)[:, None]
    page[:, unstriped(offs4)] = np.tile(f64(wgo), (H // 128, 1)) * y
    return page

@@ -1,0 +1,276 @@
+from contextlib import ExitStack
+
+import concourse.mybir as mybir
+
+K, H, T, S, T2 = 1024, 512, 4096, 1024, 2048
+FLOPS = 2 * S * H * (K + H + K)
+
+F32 = mybir.dt.float32
+BF16 = mybir.dt.bfloat16
+I32 = mybir.dt.int32
+U32 = mybir.dt.uint32
+U16 = mybir.dt.uint16
+U8 = mybir.dt.uint8
+FP8X4 = mybir.dt.float8_e4m3fn_x4
+FP4X4 = mybir.dt.float4_e2m1fn_x4
+ACT = mybir.ActivationFunctionType
+ALU = mybir.AluOpType
+
+P = 128
+PACK = 4
+K_PASS = P * PACK
+PASSES = K // K_PASS
+HALF = 512
+HALVES = S // HALF
+QUAD = 32
+QUAD_ORDER = (0, 2, 1, 3)
+
+
+def tile_list_wheel_friction_page_kernel(
+    tc, tab_words, tab_scales, offs, offs2, offs3, offs4, w1, lim, page0, wgs, bias,
+    w2_words, w2_scales, w3, gain, wgo, out,
+):
+    nc = tc.nc
+    with ExitStack() as ctx:
+        lists = ctx.enter_context(tc.tile_pool(name="lists", bufs=1))
+        keep = ctx.enter_context(tc.tile_pool(name="keep", bufs=1))
+        stage = ctx.enter_context(tc.tile_pool(name="stage", bufs=2))
+        psum = ctx.enter_context(tc.psum_pool(name="psum", bufs=1))
+
+        def cols(h):
+            return slice(h * HALF, (h + 1) * HALF)
+
+        def entries(list_tile, h):
+            return list_tile[:, h * HALF // 16 : (h + 1) * HALF // 16]
+
+        def load_list(src, name):
+            buf = lists.tile([P, S // 16], U16, name=name)
+            nc.sync.dma_start(buf[:], src)
+            return buf
+
+        def load_dealt(dst, src, engines):
+            for g in QUAD_ORDER:
+                engines[g].dma_start(out=dst[g * QUAD : (g + 1) * QUAD], in_=src)
+
+        lim_rows = lim.rearrange("(p t) j -> t p j", t=PACK)
+        page_rows = page0.rearrange("(p t) c -> t p c", t=PACK)
+        out_rows = out.rearrange("(p t) c -> t p c", t=PACK)
+        wgs_rows = wgs.rearrange("(q t) j -> q t j", t=PACK)
+        wgo_rows = wgo.rearrange("(q t) j -> q t j", t=PACK)
+        on_sync = [nc.sync] * 4
+
+        tab_sc = keep.tile([P, T], U8, name="tab_sc", align_bytes=64)
+        nc.vector.memset(tab_sc[:].bitcast(I32), 0)
+        w2_sc_raw = keep.tile([P, H], U8, name="w2_sc_raw", align_bytes=64)
+        nc.vector.memset(w2_sc_raw[:].bitcast(I32), 0)
+        for g in range(4):
+            nc.gpsimd.dma_start(
+                out=tab_sc[g * QUAD : g * QUAD + 4 * PASSES, :].bitcast(I32),
+                in_=tab_scales[:, 4 * g : 4 * g + 4, :].bitcast(I32),
+            )
+        for g in range(4):
+            nc.gpsimd.dma_start(
+                out=w2_sc_raw[g * QUAD : g * QUAD + 4, :].bitcast(I32),
+                in_=w2_scales[0, 4 * g : 4 * g + 4, :].bitcast(I32),
+            )
+
+        idx = load_list(offs, "idx")
+        idx2 = load_list(offs2, "idx2")
+        wgs0 = [keep.tile([P, HALF], F32, name="wgs0_%d" % h) for h in range(HALVES)]
+        load_dealt(wgs0[0], wgs_rows[:, 0, cols(0)], [nc.sync, nc.sync, nc.scalar, nc.scalar])
+
+        def load_tab(a):
+            buf = keep.tile([P, T], U32, name="tab_w%d" % a, align_bytes=64)
+            nc.sync.dma_start(
+                out=buf[:].bitcast(I32),
+                in_=tab_words[a].rearrange("p c i -> p (c i)").bitcast(I32),
+            )
+            return buf
+
+        def load_weight(w, a):
+            raw = stage.tile([P, PACK, H], F32, name="w_raw")
+            nc.sync.dma_start(
+                out=raw[:], in_=w[a * K_PASS : (a + 1) * K_PASS, :].rearrange("(p i) c -> p i c", i=PACK)
+            )
+            return raw
+
+        def load_rows(rows, width, name):
+            buf = keep.tile([P, width], F32, name=name)
+            nc.sync.dma_start(out=buf[:], in_=rows)
+            return buf
+
+        tab_w = [load_tab(0)]
+        w1_raw = [load_weight(w1, a) for a in range(PASSES)]
+        tab_w.append(load_tab(1))
+        lim0 = [load_rows(lim_rows[0][:, cols(0)], HALF, "lim0_0")]
+        page = [load_rows(page_rows[0], T2, "page0")]
+        lim0.append(load_rows(lim_rows[0][:, cols(1)], HALF, "lim0_1"))
+        load_dealt(wgs0[1], wgs_rows[:, 0, cols(1)], on_sync)
+
+        page.append(load_rows(page_rows[1], T2, "page1"))
+        lim_t = {1: load_rows(lim_rows[1], S, "lim1")}
+        wgs1 = keep.tile([P, S], F32, name="wgs1")
+        load_dealt(wgs1, wgs_rows[:, 1, :], on_sync)
+        idx3 = load_list(offs3, "idx3")
+        bias_t = keep.tile([P, PACK], F32, name="bias_t")
+        nc.sync.dma_start(out=bias_t[:], in_=bias.rearrange("(p t) -> p t", t=PACK))
+
+        page.append(load_rows(page_rows[2], T2, "page2"))
+        lim_t[2] = load_rows(lim_rows[2], S, "lim2")
+        wgs23 = keep.tile([P, 2, S], F32, name="wgs23")
+        load_dealt(wgs23, wgs_rows[:, 2:4, :], on_sync)
+        w2_raw = keep.tile([P, H], U16, name="w2_raw", align_bytes=64)
+        nc.sync.dma_start(out=w2_raw[:].bitcast(I32), in_=w2_words[0].bitcast(I32))
+
+        v_sc = keep.tile([P, S], U8, name="v_sc", align_bytes=64)
+        nc.vector.tensor_copy(v_sc[:], tab_sc[:].indirect(idx[:]))
+        v_w = [keep.tile([P, S], U32, name="v_w%d" % a, align_bytes=64) for a in range(PASSES)]
+        nc.vector.tensor_copy(v_w[0][:], tab_w[0][:].indirect(idx[:]))
+
+        def round_weight(raw, copy):
+            grouped = stage.tile([P, PACK * H], BF16, name="w_bf", align_bytes=64)
+            copy(
+                out=grouped[:].rearrange("p (t m i) -> p m t i", t=PACK, i=PACK),
+                in_=raw[:].rearrange("p i (m t) -> p m t i", t=PACK),
+            )
+            return grouped
+
+        def quantise(grouped, name, tag=""):
+            width = grouped.shape[1] // PACK
+            codes = keep.tile([P, width], U32, name=name + "_codes", tag=tag, align_bytes=64)
+            scales = keep.tile([P, width], U8, name=name + "_scales", align_bytes=64)
+            nc.vector.quantize_mx(out=codes[:].bitcast(FP8X4), scales=scales[:], in_=grouped[:])
+            return codes, scales
+
+        w1_bf = [round_weight(w1_raw[0], nc.scalar.copy), round_weight(w1_raw[1], nc.vector.tensor_copy)]
+        w1_q = [quantise(w1_bf[a], "w1_%d" % a) for a in range(PASSES)]
+
+        w2_sc = keep.tile([P, H], U8, name="w2_sc", align_bytes=64)
+        nc.vector.tensor_copy(
+            out=w2_sc[:].rearrange("p (t m) -> p t m", t=PACK),
+            in_=w2_sc_raw[:].rearrange("p (m t) -> p t m", t=PACK),
+        )
+        for h in range(HALVES):
+            nc.vector.tensor_copy(v_w[1][:, cols(h)], tab_w[1][:].indirect(entries(idx, h)))
+
+        w3_raw = [load_weight(w3, a) for a in range(PASSES)]
+        lim_t[3] = load_rows(lim_rows[3], S, "lim3")
+        page.append(load_rows(page_rows[3], T2, "page3"))
+        gain_t = keep.tile([P, PACK], F32, name="gain_t")
+        nc.sync.dma_start(out=gain_t[:], in_=gain.rearrange("(p t) -> p t", t=PACK))
+        idx4 = load_list(offs4, "idx4")
+        wgo_t = keep.tile([P, PACK, S], F32, name="wgo_t")
+        load_dealt(wgo_t, wgo_rows, on_sync)
+
+        def table_passes(acc, w_q, t, h, stop):
+            for a in range(PASSES):
+                codes, scales = w_q[a]
+                nc.tensor.matmul_mx(
+                    out=acc[:],
+                    lhsT=codes[:, t * P : (t + 1) * P].bitcast(FP8X4),
+                    lhsT_scale=scales[:, t * P : (t + 1) * P],
+                    rhs=v_w[a][:, cols(h)].bitcast(FP8X4),
+                    rhs_scale=v_sc[4 * a :, cols(h)],
+                    start=(a == 0),
+                    stop=(stop and a == PASSES - 1),
+                )
+
+        def bank(t, h):
+            return psum.tile([P, HALF], F32, name="bank%d%d" % (t, h))
+
+        h_acc = {}
+        for t in range(PACK):
+            for h in range(HALVES):
+                h_acc[t, h] = bank(t, h)
+                table_passes(h_acc[t, h], w1_q, t, h, True)
+
+        h_min = [keep.tile([P, S], F32, name="h_min%d" % t) for t in range(PACK)]
+        x_woven = [keep.tile([P, PACK * HALF], BF16, name="x_woven%d" % h, tag="x_woven%d" % h, align_bytes=64) for h in range(HALVES)]
+
+        def fetch(dst, t, h):
+            nc.vector.tensor_copy(dst, page[t][:].indirect(entries(idx3, h)))
+
+        def add_bias(dst, src, t):
+            nc.scalar.activation(out=dst, in_=src, func=ACT.Identity, bias=bias_t[:, t : t + 1])
+
+        def fetch_first_half(dst, t):
+            fetch(dst, t, 0)
+            add_bias(x_woven[0][:].rearrange("p (c i) -> p i c", i=PACK)[:, t, :], dst, t)
+
+        for h in range(HALVES):
+            nc.vector.tensor_tensor(h_min[0][:, cols(h)], h_acc[0, h][:], lim0[h][:], ALU.min)
+            nc.vector.tensor_tensor(
+                page[0][:].indirect(entries(idx2, h)), h_min[0][:, cols(h)], wgs0[h][:], ALU.mult
+            )
+        wgs_of = {1: wgs1[:], 2: wgs23[:, 0, :], 3: wgs23[:, 1, :]}
+        w3_q = None
+        y_acc = {}
+        for t in range(1, PACK):
+            if t == PACK - 1:
+                w2_w = keep.tile([P, H], U16, name="w2_w", align_bytes=64)
+                nc.scalar.copy(
+                    out=w2_w[:].rearrange("p (t m) -> p t m", t=PACK),
+                    in_=w2_raw[:].rearrange("p (m t) -> p t m", t=PACK),
+                )
+                w3_q = [quantise(round_weight(w3_raw[a], nc.scalar.copy), "w3_%d" % a) for a in range(PASSES)]
+            for h in range(HALVES):
+                nc.vector.tensor_tensor(h_min[t][:, cols(h)], h_acc[t, h][:], lim_t[t][:, cols(h)], ALU.min)
+            fetch_first_half(lim_t[t][:, cols(0)], t - 1)
+            nc.vector.tensor_tensor(page[t][:].indirect(idx2[:]), h_min[t][:], wgs_of[t], ALU.mult)
+        for h in range(HALVES):
+            for t in range(PACK):
+                y_acc[t, h] = bank(t, h)
+                table_passes(y_acc[t, h], w3_q, t, h, False)
+
+        def close_sums(x_q, h):
+            codes, scales = x_q
+            for t in range(PACK):
+                nc.tensor.matmul_mx(
+                    out=y_acc[t, h][:],
+                    lhsT=w2_w[:, t * P : (t + 1) * P].bitcast(FP4X4),
+                    lhsT_scale=w2_sc[:, t * P : (t + 1) * P],
+                    rhs=codes[:].bitcast(FP8X4),
+                    rhs_scale=scales[:],
+                    start=False,
+                    stop=True,
+                )
+
+        y = {}
+
+        def finish_y(t, h):
+            y[t, h] = keep.tile([P, HALF], F32, name="y%d%d" % (t, h), tag="y%d%d" % (t, h), align_bytes=64)
+            nc.scalar.activation(out=y[t, h][:], in_=y_acc[t, h][:], func=ACT.Abs)
+            nc.scalar.activation(out=y[t, h][:], in_=y[t, h][:], func=ACT.Copy, scale=gain_t[:, t : t + 1])
+
+        def put_y(t, h):
+            nc.vector.tensor_tensor(
+                page[t][:].indirect(entries(idx4, h)), y[t, h][:], wgo_t[:, t, cols(h)], ALU.mult
+            )
+
+        x_planes = keep.tile([P, PACK, HALF], BF16, name="x_planes")
+        fetch_first_half(lim0[0][:], PACK - 1)
+        for t in (0, 1):
+            fetch(h_min[PACK - 1][:, cols(t)], t, 1)
+            add_bias(x_planes[:, t, :], h_min[PACK - 1][:, cols(t)], t)
+        close_sums(quantise(x_woven[0], "x_0"), 0)
+        late = keep.tile([P, 2, HALF], F32, name="x_late", tag="x_woven0", align_bytes=64)
+        for t in (2, 3):
+            fetch(late[:, t - 2, :], t, 1)
+        finish_y(0, 0)
+        for t in (2, 3):
+            add_bias(x_planes[:, t, :], late[:, t - 2, :], t)
+        finish_y(1, 0)
+        put_y(0, 0)
+        nc.scalar.copy(
+            out=x_woven[1][:].rearrange("p (c i) -> p c i", i=PACK),
+            in_=x_planes[:].rearrange("p i c -> p c i"),
+        )
+        put_y(1, 0)
+        close_sums(quantise(x_woven[1], "x_1", tag="y00"), 1)
+        for t in (2, 3):
+            finish_y(t, 0)
+            put_y(t, 0)
+        for t in range(PACK):
+            finish_y(t, 1)
+            put_y(t, 1)
+            nc.sync.dma_start(out=out_rows[t], in_=page[t][:])

@@ -80,7 +80,7 @@ def tile_list_wheel_friction_page_kernel(
         load_dealt(wgs0[0], wgs_rows[:, 0, cols(0)], [nc.sync, nc.sync, nc.scalar, nc.scalar])
 
         def load_tab(a):
-            buf = keep.tile([P, T], U32, name="tab_w%d" % a, align_bytes=64)
+            buf = keep.tile([P, T], U32, name="tab_w%d" % a, tag="tab_w%d" % a, align_bytes=64)
             nc.sync.dma_start(
                 out=buf[:].bitcast(I32),
                 in_=tab_words[a].rearrange("p c i -> p (c i)").bitcast(I32),
@@ -99,41 +99,35 @@ def tile_list_wheel_friction_page_kernel(
             nc.sync.dma_start(out=buf[:], in_=rows)
             return buf
 
-        tab_w = [load_tab(0)]
         w1_raw = [load_weight(w1, a) for a in range(PASSES)]
-        tab_w.append(load_tab(1))
+        tab_w = [load_tab(a) for a in range(PASSES)]
         lim0 = [load_rows(lim_rows[0][:, cols(0)], HALF, "lim0_0")]
         page = [load_rows(page_rows[0], T2, "page0")]
         lim0.append(load_rows(lim_rows[0][:, cols(1)], HALF, "lim0_1"))
         load_dealt(wgs0[1], wgs_rows[:, 0, cols(1)], on_sync)
 
-        page.append(load_rows(page_rows[1], T2, "page1"))
-        lim_t = {1: load_rows(lim_rows[1], S, "lim1")}
-        wgs1 = keep.tile([P, S], F32, name="wgs1")
-        load_dealt(wgs1, wgs_rows[:, 1, :], on_sync)
+        lim_t, wgs_t = {}, {}
+
+        def load_tile_inputs(t):
+            lim_t[t] = load_rows(lim_rows[t], S, "lim%d" % t)
+            wgs_t[t] = keep.tile([P, S], F32, name="wgs%d" % t, tag="wgs%d" % t, align_bytes=64)
+            load_dealt(wgs_t[t], wgs_rows[:, t, :], on_sync)
+            page.append(load_rows(page_rows[t], T2, "page%d" % t))
+
         idx3 = load_list(offs3, "idx3")
+        load_tile_inputs(1)
         bias_t = keep.tile([P, PACK], F32, name="bias_t")
         nc.sync.dma_start(out=bias_t[:], in_=bias.rearrange("(p t) -> p t", t=PACK))
 
-        page.append(load_rows(page_rows[2], T2, "page2"))
-        lim_t[2] = load_rows(lim_rows[2], S, "lim2")
-        wgs23 = keep.tile([P, 2, S], F32, name="wgs23")
-        load_dealt(wgs23, wgs_rows[:, 2:4, :], on_sync)
+        load_tile_inputs(2)
         w2_raw = keep.tile([P, H], U16, name="w2_raw", align_bytes=64)
         nc.sync.dma_start(out=w2_raw[:].bitcast(I32), in_=w2_words[0].bitcast(I32))
 
-        v_sc = keep.tile([P, S], U8, name="v_sc", align_bytes=64)
-        nc.vector.tensor_copy(v_sc[:], tab_sc[:].indirect(idx[:]))
-        v_w = [keep.tile([P, S], U32, name="v_w%d" % a, align_bytes=64) for a in range(PASSES)]
-        nc.vector.tensor_copy(v_w[0][:], tab_w[0][:].indirect(idx[:]))
-
-        def round_weight(raw, copy):
-            grouped = stage.tile([P, PACK * H], BF16, name="w_bf", align_bytes=64)
+        def round_weight(dst, raw, copy):
             copy(
-                out=grouped[:].rearrange("p (t m i) -> p m t i", t=PACK, i=PACK),
+                out=dst.rearrange("p (t m i) -> p m t i", t=PACK, i=PACK),
                 in_=raw[:].rearrange("p i (m t) -> p m t i", t=PACK),
             )
-            return grouped
 
         def quantise(grouped, name, tag=""):
             width = grouped.shape[1] // PACK
@@ -142,10 +136,17 @@ def tile_list_wheel_friction_page_kernel(
             nc.vector.quantize_mx(out=codes[:].bitcast(FP8X4), scales=scales[:], in_=grouped[:])
             return codes, scales
 
-        w1_bf = [round_weight(w1_raw[0], nc.scalar.copy), round_weight(w1_raw[1], nc.vector.tensor_copy)]
-        w1_q = [quantise(w1_bf[a], "w1_%d" % a) for a in range(PASSES)]
+        w1_q = []
+        for a, copy in enumerate((nc.scalar.copy, nc.vector.tensor_copy)):
+            w1_bf = keep.tile([P, PACK * H], BF16, name="w1_bf%d" % a, tag="w1_bf%d" % a, align_bytes=64)
+            round_weight(w1_bf[:], w1_raw[a], copy)
+            w1_q.append(quantise(w1_bf, "w1_%d" % a))
 
-        w2_sc = keep.tile([P, H], U8, name="w2_sc", align_bytes=64)
+        v_sc = keep.tile([P, S], U8, name="v_sc", tag="w1_bf1", align_bytes=64)
+        nc.vector.tensor_copy(v_sc[:], tab_sc[:].indirect(idx[:]))
+        v_w = [keep.tile([P, S], U32, name="v_w%d" % a, align_bytes=64) for a in range(PASSES)]
+        nc.vector.tensor_copy(v_w[0][:], tab_w[0][:].indirect(idx[:]))
+        w2_sc = keep.tile([P, H], U8, name="w2_sc", tag="tab_w0", align_bytes=64)
         nc.vector.tensor_copy(
             out=w2_sc[:].rearrange("p (t m) -> p t m", t=PACK),
             in_=w2_sc_raw[:].rearrange("p (m t) -> p t m", t=PACK),
@@ -154,26 +155,26 @@ def tile_list_wheel_friction_page_kernel(
             nc.vector.tensor_copy(v_w[1][:, cols(h)], tab_w[1][:].indirect(entries(idx, h)))
 
         w3_raw = [load_weight(w3, a) for a in range(PASSES)]
-        lim_t[3] = load_rows(lim_rows[3], S, "lim3")
-        page.append(load_rows(page_rows[3], T2, "page3"))
+        load_tile_inputs(3)
         gain_t = keep.tile([P, PACK], F32, name="gain_t")
         nc.sync.dma_start(out=gain_t[:], in_=gain.rearrange("(p t) -> p t", t=PACK))
         idx4 = load_list(offs4, "idx4")
-        wgo_t = keep.tile([P, PACK, S], F32, name="wgo_t")
-        load_dealt(wgo_t, wgo_rows, on_sync)
+        wgo_t = []
+        for u in range(2):
+            wgo_t.append(keep.tile([P, 2, S], F32, name="wgo%d" % u))
+            load_dealt(wgo_t[u], wgo_rows[:, 2 * u : 2 * u + 2, :], on_sync)
 
-        def table_passes(acc, w_q, t, h, stop):
-            for a in range(PASSES):
-                codes, scales = w_q[a]
-                nc.tensor.matmul_mx(
-                    out=acc[:],
-                    lhsT=codes[:, t * P : (t + 1) * P].bitcast(FP8X4),
-                    lhsT_scale=scales[:, t * P : (t + 1) * P],
-                    rhs=v_w[a][:, cols(h)].bitcast(FP8X4),
-                    rhs_scale=v_sc[4 * a :, cols(h)],
-                    start=(a == 0),
-                    stop=(stop and a == PASSES - 1),
-                )
+        def table_pass(acc, w_q, a, t, h, start, stop):
+            codes, scales = w_q[a]
+            nc.tensor.matmul_mx(
+                out=acc[:],
+                lhsT=codes[:, t * P : (t + 1) * P].bitcast(FP8X4),
+                lhsT_scale=scales[:, t * P : (t + 1) * P],
+                rhs=v_w[a][:, cols(h)].bitcast(FP8X4),
+                rhs_scale=v_sc[4 * a :, cols(h)],
+                start=start,
+                stop=stop,
+            )
 
         def bank(t, h):
             return psum.tile([P, HALF], F32, name="bank%d%d" % (t, h))
@@ -182,7 +183,9 @@ def tile_list_wheel_friction_page_kernel(
         for t in range(PACK):
             for h in range(HALVES):
                 h_acc[t, h] = bank(t, h)
-                table_passes(h_acc[t, h], w1_q, t, h, True)
+                first = 0 if t == 0 else 1
+                table_pass(h_acc[t, h], w1_q, first, t, h, True, False)
+                table_pass(h_acc[t, h], w1_q, 1 - first, t, h, False, True)
 
         h_min = [keep.tile([P, S], F32, name="h_min%d" % t) for t in range(PACK)]
         x_woven = [keep.tile([P, PACK * HALF], BF16, name="x_woven%d" % h, tag="x_woven%d" % h, align_bytes=64) for h in range(HALVES)]
@@ -202,9 +205,7 @@ def tile_list_wheel_friction_page_kernel(
             nc.vector.tensor_tensor(
                 page[0][:].indirect(entries(idx2, h)), h_min[0][:, cols(h)], wgs0[h][:], ALU.mult
             )
-        wgs_of = {1: wgs1[:], 2: wgs23[:, 0, :], 3: wgs23[:, 1, :]}
-        w3_q = None
-        y_acc = {}
+        w3_bf = keep.tile([P, PASSES * PACK * H], BF16, name="w3_bf", align_bytes=64)
         for t in range(1, PACK):
             if t == PACK - 1:
                 w2_w = keep.tile([P, H], U16, name="w2_w", align_bytes=64)
@@ -212,65 +213,76 @@ def tile_list_wheel_friction_page_kernel(
                     out=w2_w[:].rearrange("p (t m) -> p t m", t=PACK),
                     in_=w2_raw[:].rearrange("p (m t) -> p t m", t=PACK),
                 )
-                w3_q = [quantise(round_weight(w3_raw[a], nc.scalar.copy), "w3_%d" % a) for a in range(PASSES)]
+                for a in range(PASSES):
+                    round_weight(w3_bf[:, a * PACK * H : (a + 1) * PACK * H], w3_raw[a], nc.scalar.copy)
             for h in range(HALVES):
                 nc.vector.tensor_tensor(h_min[t][:, cols(h)], h_acc[t, h][:], lim_t[t][:, cols(h)], ALU.min)
             fetch_first_half(lim_t[t][:, cols(0)], t - 1)
-            nc.vector.tensor_tensor(page[t][:].indirect(idx2[:]), h_min[t][:], wgs_of[t], ALU.mult)
-        for h in range(HALVES):
-            for t in range(PACK):
-                y_acc[t, h] = bank(t, h)
-                table_passes(y_acc[t, h], w3_q, t, h, False)
+            nc.vector.tensor_tensor(page[t][:].indirect(idx2[:]), h_min[t][:], wgs_t[t][:], ALU.mult)
 
-        def close_sums(x_q, h):
+        y_acc = {}
+
+        def second_sums(w3_q, x_q, h):
             codes, scales = x_q
             for t in range(PACK):
+                acc = bank(t, h)
+                y_acc[t, h] = acc
+                table_first = (t, h) == (0, 0)
+                if table_first:
+                    table_pass(acc, w3_q, 0, t, h, True, False)
+                    table_pass(acc, w3_q, 1, t, h, False, False)
                 nc.tensor.matmul_mx(
-                    out=y_acc[t, h][:],
+                    out=acc[:],
                     lhsT=w2_w[:, t * P : (t + 1) * P].bitcast(FP4X4),
                     lhsT_scale=w2_sc[:, t * P : (t + 1) * P],
                     rhs=codes[:].bitcast(FP8X4),
                     rhs_scale=scales[:],
-                    start=False,
-                    stop=True,
+                    start=not table_first,
+                    stop=table_first,
                 )
+                if not table_first:
+                    table_pass(acc, w3_q, 0, t, h, False, False)
+                    table_pass(acc, w3_q, 1, t, h, False, True)
 
         y = {}
 
-        def finish_y(t, h):
-            y[t, h] = keep.tile([P, HALF], F32, name="y%d%d" % (t, h), tag="y%d%d" % (t, h), align_bytes=64)
-            nc.scalar.activation(out=y[t, h][:], in_=y_acc[t, h][:], func=ACT.Abs)
-            nc.scalar.activation(out=y[t, h][:], in_=y[t, h][:], func=ACT.Copy, scale=gain_t[:, t : t + 1])
+        def finish_y(t, h, tag, bufs, magnitude):
+            y[t, h] = keep.tile([P, HALF], F32, name="y%d%d" % (t, h), tag=tag, bufs=bufs, align_bytes=64)
+            nc.scalar.activation(out=magnitude, in_=y_acc[t, h][:], func=ACT.Abs)
+            nc.scalar.activation(out=y[t, h][:], in_=magnitude, func=ACT.Copy, scale=gain_t[:, t : t + 1])
 
         def put_y(t, h):
             nc.vector.tensor_tensor(
-                page[t][:].indirect(entries(idx4, h)), y[t, h][:], wgo_t[:, t, cols(h)], ALU.mult
+                page[t][:].indirect(entries(idx4, h)), y[t, h][:], wgo_t[t // 2][:, t % 2, cols(h)], ALU.mult
             )
 
-        x_planes = keep.tile([P, PACK, HALF], BF16, name="x_planes")
+        x_planes = keep.tile([P, PACK * HALF], BF16, name="x_planes", align_bytes=64)
         fetch_first_half(lim0[0][:], PACK - 1)
-        for t in (0, 1):
-            fetch(h_min[PACK - 1][:, cols(t)], t, 1)
-            add_bias(x_planes[:, t, :], h_min[PACK - 1][:, cols(t)], t)
-        close_sums(quantise(x_woven[0], "x_0"), 0)
+        fetch(h_min[PACK - 1][:, cols(0)], 0, 1)
+        add_bias(x_planes[:, cols(0)], h_min[PACK - 1][:, cols(0)], 0)
+        w3_codes, w3_scales = quantise(w3_bf, "w3", tag="wgs3")
+        w3_q = [(w3_codes[:, a * H : (a + 1) * H], w3_scales[:, a * H : (a + 1) * H]) for a in range(PASSES)]
+        second_sums(w3_q, quantise(x_woven[0], "x_0"), 0)
+        fetch(h_min[PACK - 1][:, cols(1)], 1, 1)
+        add_bias(x_planes[:, cols(1)], h_min[PACK - 1][:, cols(1)], 1)
         late = keep.tile([P, 2, HALF], F32, name="x_late", tag="x_woven0", align_bytes=64)
         for t in (2, 3):
             fetch(late[:, t - 2, :], t, 1)
-        finish_y(0, 0)
+        finish_y(0, 0, "y00", 1, x_planes[:, 2 * HALF :].bitcast(F32))
         for t in (2, 3):
-            add_bias(x_planes[:, t, :], late[:, t - 2, :], t)
-        finish_y(1, 0)
+            add_bias(x_planes[:, cols(t)], late[:, t - 2, :], t)
+        finish_y(1, 0, "y10", 1, x_woven[1][:, : 2 * HALF].bitcast(F32))
         put_y(0, 0)
         nc.scalar.copy(
             out=x_woven[1][:].rearrange("p (c i) -> p c i", i=PACK),
-            in_=x_planes[:].rearrange("p i c -> p c i"),
+            in_=x_planes[:].rearrange("p (i c) -> p c i", i=PACK),
         )
         put_y(1, 0)
-        close_sums(quantise(x_woven[1], "x_1", tag="y00"), 1)
+        second_sums(w3_q, quantise(x_woven[1], "x_1", tag="y00"), 1)
         for t in (2, 3):
-            finish_y(t, 0)
+            finish_y(t, 0, "y_ring", 2, h_min[0][:, cols(t - 2)])
             put_y(t, 0)
         for t in range(PACK):
-            finish_y(t, 1)
+            finish_y(t, 1, "y_ring", 2, h_min[1 + t // 2][:, cols(t % 2)])
             put_y(t, 1)
             nc.sync.dma_start(out=out_rows[t], in_=page[t][:])

@@ -63,21 +63,13 @@ def tile_list_wheel_friction_page_kernel(
         nc.vector.memset(tab_sc[:].bitcast(I32), 0)
         w2_sc_raw = keep.tile([P, H], U8, name="w2_sc_raw", align_bytes=64)
         nc.vector.memset(w2_sc_raw[:].bitcast(I32), 0)
-        for g in range(4):
-            nc.gpsimd.dma_start(
+        for g in QUAD_ORDER:
+            nc.sync.dma_start(
                 out=tab_sc[g * QUAD : g * QUAD + 4 * PASSES, :].bitcast(I32),
                 in_=tab_scales[:, 4 * g : 4 * g + 4, :].bitcast(I32),
             )
-        for g in range(4):
-            nc.gpsimd.dma_start(
-                out=w2_sc_raw[g * QUAD : g * QUAD + 4, :].bitcast(I32),
-                in_=w2_scales[0, 4 * g : 4 * g + 4, :].bitcast(I32),
-            )
 
         idx = load_list(offs, "idx")
-        idx2 = load_list(offs2, "idx2")
-        wgs0 = [keep.tile([P, HALF], F32, name="wgs0_%d" % h) for h in range(HALVES)]
-        load_dealt(wgs0[0], wgs_rows[:, 0, cols(0)], [nc.sync, nc.sync, nc.scalar, nc.scalar])
 
         def load_tab(a):
             buf = keep.tile([P, T], U32, name="tab_w%d" % a, tag="tab_w%d" % a, align_bytes=64)
@@ -100,7 +92,15 @@ def tile_list_wheel_friction_page_kernel(
             return buf
 
         w1_raw = [load_weight(w1, a) for a in range(PASSES)]
-        tab_w = [load_tab(a) for a in range(PASSES)]
+        w2_sc_rows = keep.tile([4, 4, H // 4], I32, name="w2_sc_rows")
+        nc.sync.dma_start(
+            out=w2_sc_rows[:], in_=w2_scales[0].bitcast(I32).rearrange("(g r) c -> r g c", r=4)
+        )
+        tab_w = [load_tab(0)]
+        idx2 = load_list(offs2, "idx2")
+        wgs0 = [keep.tile([P, HALF], F32, name="wgs0_%d" % h) for h in range(HALVES)]
+        load_dealt(wgs0[0], wgs_rows[:, 0, cols(0)], on_sync)
+        tab_w.append(load_tab(1))
         lim0 = [load_rows(lim_rows[0][:, cols(0)], HALF, "lim0_0")]
         page = [load_rows(page_rows[0], T2, "page0")]
         lim0.append(load_rows(lim_rows[0][:, cols(1)], HALF, "lim0_1"))
@@ -142,6 +142,10 @@ def tile_list_wheel_friction_page_kernel(
             round_weight(w1_bf[:], w1_raw[a], copy)
             w1_q.append(quantise(w1_bf, "w1_%d" % a))
 
+        for g in range(4):
+            nc.vector.tensor_copy(
+                out=w2_sc_raw[g * QUAD : g * QUAD + 4, :].bitcast(I32), in_=w2_sc_rows[:, g, :]
+            )
         v_sc = keep.tile([P, S], U8, name="v_sc", tag="w1_bf1", align_bytes=64)
         nc.vector.tensor_copy(v_sc[:], tab_sc[:].indirect(idx[:]))
         v_w = [keep.tile([P, S], U32, name="v_w%d" % a, align_bytes=64) for a in range(PASSES)]

@@ -1,6 +1,7 @@
 from contextlib import ExitStack
 
 import concourse.mybir as mybir
+from concourse.masks import make_identity
 
 K, H, T, S, T2 = 1024, 512, 4096, 1024, 2048
 FLOPS = 2 * S * H * (K + H + K)
@@ -20,10 +21,12 @@ P = 128
 PACK = 4
 K_PASS = P * PACK
 PASSES = K // K_PASS
+TILES = H // P
 HALF = 512
 HALVES = S // HALF
+BLOCKS = HALF // P
 QUAD = 32
-QUAD_ORDER = (0, 2, 1, 3)
+SCALE_ROWS = 4
 
 
 def tile_list_wheel_friction_page_kernel(
@@ -34,202 +37,214 @@ def tile_list_wheel_friction_page_kernel(
     with ExitStack() as ctx:
         lists = ctx.enter_context(tc.tile_pool(name="lists", bufs=1))
         keep = ctx.enter_context(tc.tile_pool(name="keep", bufs=1))
-        stage = ctx.enter_context(tc.tile_pool(name="stage", bufs=2))
         psum = ctx.enter_context(tc.psum_pool(name="psum", bufs=1))
 
         def cols(h):
             return slice(h * HALF, (h + 1) * HALF)
 
+        def rows(t):
+            return slice(t * P, (t + 1) * P)
+
         def entries(list_tile, h):
             return list_tile[:, h * HALF // 16 : (h + 1) * HALF // 16]
+
+        def sbuf(shape, dtype, name, tag=None):
+            return keep.tile(shape, dtype, name=name, tag=tag or name, align_bytes=64)
+
+        def bank(shape, dtype, t, h):
+            return psum.tile(shape, dtype, name="bank%d%d" % (t, h))
+
+        def load(src, dtype, name):
+            buf = sbuf(list(src.shape), dtype, name)
+            nc.sync.dma_start(out=buf[:], in_=src)
+            return buf
 
         def load_list(src, name):
             buf = lists.tile([P, S // 16], U16, name=name)
             nc.sync.dma_start(buf[:], src)
             return buf
 
-        def load_dealt(dst, src, engines):
-            for g in QUAD_ORDER:
-                engines[g].dma_start(out=dst[g * QUAD : (g + 1) * QUAD], in_=src)
-
-        lim_rows = lim.rearrange("(p t) j -> t p j", t=PACK)
-        page_rows = page0.rearrange("(p t) c -> t p c", t=PACK)
-        out_rows = out.rearrange("(p t) c -> t p c", t=PACK)
-        wgs_rows = wgs.rearrange("(q t) j -> q t j", t=PACK)
-        wgo_rows = wgo.rearrange("(q t) j -> q t j", t=PACK)
-        on_sync = [nc.sync] * 4
-
-        tab_sc = keep.tile([P, T], U8, name="tab_sc", align_bytes=64)
-        nc.vector.memset(tab_sc[:].bitcast(I32), 0)
-        w2_sc_raw = keep.tile([P, H], U8, name="w2_sc_raw", align_bytes=64)
-        nc.vector.memset(w2_sc_raw[:].bitcast(I32), 0)
-        for g in QUAD_ORDER:
-            nc.sync.dma_start(
-                out=tab_sc[g * QUAD : g * QUAD + 4 * PASSES, :].bitcast(I32),
-                in_=tab_scales[:, 4 * g : 4 * g + 4, :].bitcast(I32),
-            )
-
-        idx = load_list(offs, "idx")
-
-        def load_tab(a):
-            buf = keep.tile([P, T], U32, name="tab_w%d" % a, tag="tab_w%d" % a, align_bytes=64)
+        def load_table(a):
+            buf = sbuf([P, T], U32, "tab_w%d" % a)
             nc.sync.dma_start(
                 out=buf[:].bitcast(I32),
                 in_=tab_words[a].rearrange("p c i -> p (c i)").bitcast(I32),
             )
             return buf
 
-        def load_weight(w, a):
-            raw = stage.tile([P, PACK, H], F32, name="w_raw")
-            nc.sync.dma_start(
-                out=raw[:], in_=w[a * K_PASS : (a + 1) * K_PASS, :].rearrange("(p i) c -> p i c", i=PACK)
-            )
-            return raw
+        def load_weight(w, a, name):
+            return load(w[a * K_PASS : (a + 1) * K_PASS].rearrange("(p i) c -> p i c", i=PACK), F32, name)
 
-        def load_rows(rows, width, name):
-            buf = keep.tile([P, width], F32, name=name)
-            nc.sync.dma_start(out=buf[:], in_=rows)
+        def load_per_row(vec, name):
+            buf = sbuf([P, TILES], F32, name)
+            with nc.allow_non_contiguous_dma(reason="one value for each row of the page"):
+                nc.sync.dma_start(out=buf[:], in_=vec.rearrange("(t p) -> p t", p=P))
             return buf
 
-        w1_raw = [load_weight(w1, a) for a in range(PASSES)]
-        w2_sc_rows = keep.tile([4, 4, H // 4], I32, name="w2_sc_rows")
-        nc.sync.dma_start(
-            out=w2_sc_rows[:], in_=w2_scales[0].bitcast(I32).rearrange("(g r) c -> r g c", r=4)
-        )
-        tab_w = [load_tab(0)]
-        idx2 = load_list(offs2, "idx2")
-        wgs0 = [keep.tile([P, HALF], F32, name="wgs0_%d" % h) for h in range(HALVES)]
-        load_dealt(wgs0[0], wgs_rows[:, 0, cols(0)], on_sync)
-        tab_w.append(load_tab(1))
-        lim0 = [load_rows(lim_rows[0][:, cols(0)], HALF, "lim0_0")]
-        page = [load_rows(page_rows[0], T2, "page0")]
-        lim0.append(load_rows(lim_rows[0][:, cols(1)], HALF, "lim0_1"))
-        load_dealt(wgs0[1], wgs_rows[:, 0, cols(1)], on_sync)
+        ident_bf = sbuf([P, P], BF16, "ident_bf")
+        make_identity(nc, ident_bf[:])
+        ident_f32 = sbuf([P, P], F32, "ident_f32")
+        make_identity(nc, ident_f32[:])
 
-        lim_t, wgs_t = {}, {}
+        tab_sc = sbuf([P, T], U8, "tab_sc")
+        nc.vector.memset(tab_sc[:].bitcast(I32), 0)
+        w2_sc = sbuf([P, H], U8, "w2_sc")
+        nc.vector.memset(w2_sc[:].bitcast(I32), 0)
+        for g in (0, 2, 1, 3):
+            nc.sync.dma_start(
+                out=tab_sc[g * QUAD : g * QUAD + SCALE_ROWS * PASSES, :].bitcast(I32),
+                in_=tab_scales[:, SCALE_ROWS * g : SCALE_ROWS * (g + 1), :].bitcast(I32),
+            )
+
+        idx = load_list(offs, "idx")
+        w1_early = [load_weight(w1[:, : H // 2], a, "w1_early%d" % a) for a in range(PASSES)]
+        w2_sc_rows = load(w2_scales[0].bitcast(I32).rearrange("(g r) c -> r g c", r=SCALE_ROWS), I32, "w2_sc_rows")
+        tab_w = [load_table(0)]
+        idx2 = load_list(offs2, "idx2")
+        tab_w.append(load_table(1))
+        lim0 = [load(lim[rows(0), cols(0)], F32, "lim0_0")]
+        wgs_t = sbuf([P, S], F32, "wgs_t")
+        nc.sync.dma_start(out=wgs_t[:, cols(0)], in_=wgs[:, cols(0)])
+        page = [load(page0[rows(0), :], F32, "page0")]
+        lim0.append(load(lim[rows(0), cols(1)], F32, "lim0_1"))
+        nc.sync.dma_start(out=wgs_t[:, cols(1)], in_=wgs[:, cols(1)])
+        lim_t = {}
 
         def load_tile_inputs(t):
-            lim_t[t] = load_rows(lim_rows[t], S, "lim%d" % t)
-            wgs_t[t] = keep.tile([P, S], F32, name="wgs%d" % t, tag="wgs%d" % t, align_bytes=64)
-            load_dealt(wgs_t[t], wgs_rows[:, t, :], on_sync)
-            page.append(load_rows(page_rows[t], T2, "page%d" % t))
+            lim_t[t] = load(lim[rows(t), :], F32, "lim%d" % t)
+            page.append(load(page0[rows(t), :], F32, "page%d" % t))
 
+        w1_late = [load_weight(w1[:, H // 2 :], a, "w1_late%d" % a) for a in range(PASSES)]
         idx3 = load_list(offs3, "idx3")
         load_tile_inputs(1)
-        bias_t = keep.tile([P, PACK], F32, name="bias_t")
-        nc.sync.dma_start(out=bias_t[:], in_=bias.rearrange("(p t) -> p t", t=PACK))
-
+        bias_t = load_per_row(bias, "bias_t")
+        gain_t = load_per_row(gain, "gain_t")
+        wgo_t = load(wgo, F32, "wgo_t")
         load_tile_inputs(2)
-        w2_raw = keep.tile([P, H], U16, name="w2_raw", align_bytes=64)
-        nc.sync.dma_start(out=w2_raw[:].bitcast(I32), in_=w2_words[0].bitcast(I32))
+        w2_w = sbuf([P, 2 * H], U8, "w2_w")
+        nc.sync.dma_start(out=w2_w[:].bitcast(I32), in_=w2_words[0].bitcast(I32))
 
         def round_weight(dst, raw, copy):
             copy(
-                out=dst.rearrange("p (t m i) -> p m t i", t=PACK, i=PACK),
-                in_=raw[:].rearrange("p i (m t) -> p m t i", t=PACK),
+                out=dst.rearrange("p (c e i) -> p c i e", e=4, i=PACK),
+                in_=raw[:].rearrange("p i (c e) -> p c i e", e=4),
             )
 
-        def quantise(grouped, name, tag=""):
+        def quantise(grouped, name, tag=None):
             width = grouped.shape[1] // PACK
-            codes = keep.tile([P, width], U32, name=name + "_codes", tag=tag, align_bytes=64)
-            scales = keep.tile([P, width], U8, name=name + "_scales", align_bytes=64)
+            codes = sbuf([P, width], U32, name + "_codes", tag)
+            scales = sbuf([P, width], U8, name + "_scales")
             nc.vector.quantize_mx(out=codes[:].bitcast(FP8X4), scales=scales[:], in_=grouped[:])
             return codes, scales
 
-        w1_q = []
-        for a, copy in enumerate((nc.scalar.copy, nc.vector.tensor_copy)):
-            w1_bf = keep.tile([P, PACK * H], BF16, name="w1_bf%d" % a, tag="w1_bf%d" % a, align_bytes=64)
-            round_weight(w1_bf[:], w1_raw[a], copy)
-            w1_q.append(quantise(w1_bf, "w1_%d" % a))
+        def stationary(quantised, first):
+            codes, scales = quantised
+            return codes[:, first : first + P], scales[:, first : first + P]
 
-        for g in range(4):
+        w1_q = {}
+        for a, copy in enumerate((nc.scalar.copy, nc.vector.tensor_copy)):
+            w1_bf = sbuf([P, PACK * H // 2], BF16, "w1_bf%d" % a)
+            round_weight(w1_bf[:], w1_early[a], copy)
+            early = quantise(w1_bf, "w1_early%d" % a)
+            for t in range(TILES // 2):
+                w1_q[a, t] = stationary(early, t * P)
+
+        for g in range(P // QUAD):
             nc.vector.tensor_copy(
-                out=w2_sc_raw[g * QUAD : g * QUAD + 4, :].bitcast(I32), in_=w2_sc_rows[:, g, :]
+                out=w2_sc[g * QUAD : g * QUAD + SCALE_ROWS, :].bitcast(I32), in_=w2_sc_rows[:, g, :]
             )
-        v_sc = keep.tile([P, S], U8, name="v_sc", tag="w1_bf1", align_bytes=64)
+        v_sc = sbuf([P, S], U8, "v_sc", "w1_bf1")
         nc.vector.tensor_copy(v_sc[:], tab_sc[:].indirect(idx[:]))
-        v_w = [keep.tile([P, S], U32, name="v_w%d" % a, align_bytes=64) for a in range(PASSES)]
+        v_w = [sbuf([P, S], U32, "v_w%d" % a) for a in range(PASSES)]
         nc.vector.tensor_copy(v_w[0][:], tab_w[0][:].indirect(idx[:]))
-        w2_sc = keep.tile([P, H], U8, name="w2_sc", tag="tab_w0", align_bytes=64)
-        nc.vector.tensor_copy(
-            out=w2_sc[:].rearrange("p (t m) -> p t m", t=PACK),
-            in_=w2_sc_raw[:].rearrange("p (m t) -> p t m", t=PACK),
-        )
         for h in range(HALVES):
             nc.vector.tensor_copy(v_w[1][:, cols(h)], tab_w[1][:].indirect(entries(idx, h)))
 
-        w3_raw = [load_weight(w3, a) for a in range(PASSES)]
+        w1_late_bf = sbuf([P, PASSES, PACK * H // 2], BF16, "w1_late_bf")
+        for a in range(PASSES):
+            round_weight(w1_late_bf[:, a, :], w1_late[a], nc.scalar.copy)
+        late = quantise(w1_late_bf[:].rearrange("p a c -> p (a c)"), "w1_late")
+        for a in range(PASSES):
+            for t in range(TILES // 2):
+                w1_q[a, TILES // 2 + t] = stationary(late, a * H // 2 + t * P)
+
+        w3_raw = [load_weight(w3, a, "w3_raw%d" % a) for a in range(PASSES)]
         load_tile_inputs(3)
-        gain_t = keep.tile([P, PACK], F32, name="gain_t")
-        nc.sync.dma_start(out=gain_t[:], in_=gain.rearrange("(p t) -> p t", t=PACK))
         idx4 = load_list(offs4, "idx4")
-        wgo_t = []
-        for u in range(2):
-            wgo_t.append(keep.tile([P, 2, S], F32, name="wgo%d" % u))
-            load_dealt(wgo_t[u], wgo_rows[:, 2 * u : 2 * u + 2, :], on_sync)
 
         def table_pass(acc, w_q, a, t, h, start, stop):
-            codes, scales = w_q[a]
+            codes, scales = w_q[a, t]
             nc.tensor.matmul_mx(
                 out=acc[:],
-                lhsT=codes[:, t * P : (t + 1) * P].bitcast(FP8X4),
-                lhsT_scale=scales[:, t * P : (t + 1) * P],
+                lhsT=codes.bitcast(FP8X4),
+                lhsT_scale=scales,
                 rhs=v_w[a][:, cols(h)].bitcast(FP8X4),
-                rhs_scale=v_sc[4 * a :, cols(h)],
+                rhs_scale=v_sc[SCALE_ROWS * a :, cols(h)],
                 start=start,
                 stop=stop,
             )
 
-        def bank(t, h):
-            return psum.tile([P, HALF], F32, name="bank%d%d" % (t, h))
-
         h_acc = {}
-        for t in range(PACK):
+        for t in range(TILES):
             for h in range(HALVES):
-                h_acc[t, h] = bank(t, h)
+                h_acc[t, h] = bank([P, HALF], F32, t, h)
                 first = 0 if t == 0 else 1
                 table_pass(h_acc[t, h], w1_q, first, t, h, True, False)
                 table_pass(h_acc[t, h], w1_q, 1 - first, t, h, False, True)
 
-        h_min = [keep.tile([P, S], F32, name="h_min%d" % t) for t in range(PACK)]
-        x_woven = [keep.tile([P, PACK * HALF], BF16, name="x_woven%d" % h, tag="x_woven%d" % h, align_bytes=64) for h in range(HALVES)]
+        h_min = [sbuf([P, S], F32, "h_min%d" % t) for t in range(TILES)]
+        x_pairs = [sbuf([P, BLOCKS, 2, P], F32, "x_pairs%d" % h) for h in range(HALVES)]
 
-        def fetch(dst, t, h):
-            nc.vector.tensor_copy(dst, page[t][:].indirect(entries(idx3, h)))
+        x_bf0 = sbuf([P, TILES, HALF], BF16, "x_bf0")
 
-        def add_bias(dst, src, t):
-            nc.scalar.activation(out=dst, in_=src, func=ACT.Identity, bias=bias_t[:, t : t + 1])
+        def fetch_x(buf, t, h):
+            nc.vector.tensor_copy(buf, page[t][:].indirect(entries(idx3, h)))
 
-        def fetch_first_half(dst, t):
-            fetch(dst, t, 0)
-            add_bias(x_woven[0][:].rearrange("p (c i) -> p i c", i=PACK)[:, t, :], dst, t)
+        def turn_x(buf, x_bf, t, h):
+            nc.scalar.activation(out=x_bf, in_=buf, func=ACT.Identity, bias=bias_t[:, t : t + 1])
+            turned = bank([P, BLOCKS, P], BF16, t % 2, 1)
+            for b in range(BLOCKS):
+                nc.tensor.transpose(turned[:, b, :], x_bf[:, rows(b)], ident_bf[:])
+            nc.scalar.copy(
+                out=x_pairs[h][:, :, :, t * QUAD : (t + 1) * QUAD],
+                in_=turned[:].bitcast(F32).rearrange("j b (q u) -> j b u q", u=2),
+            )
+
+        def weave_x(h):
+            woven = sbuf([P, PACK * HALF], BF16, "x_woven%d" % h)
+            words = woven[:].bitcast(F32).rearrange("p (b j u) -> p b j u", b=BLOCKS, u=2)
+            for n in range(2):
+                back = bank([P, 2, 2, P], F32, 2 + n, 1)
+                for b in range(2):
+                    for u in range(2):
+                        nc.tensor.transpose(back[:, b, u, :], x_pairs[h][:, 2 * n + b, u, :], ident_f32[:])
+                nc.scalar.copy(out=words[:, 2 * n : 2 * n + 2], in_=back[:].rearrange("p b u j -> p b j u"))
+            return woven
 
         for h in range(HALVES):
             nc.vector.tensor_tensor(h_min[0][:, cols(h)], h_acc[0, h][:], lim0[h][:], ALU.min)
             nc.vector.tensor_tensor(
-                page[0][:].indirect(entries(idx2, h)), h_min[0][:, cols(h)], wgs0[h][:], ALU.mult
+                page[0][:].indirect(entries(idx2, h)), h_min[0][:, cols(h)], wgs_t[:, cols(h)], ALU.mult
             )
-        w3_bf = keep.tile([P, PASSES * PACK * H], BF16, name="w3_bf", align_bytes=64)
-        for t in range(1, PACK):
-            if t == PACK - 1:
-                w2_w = keep.tile([P, H], U16, name="w2_w", align_bytes=64)
-                nc.scalar.copy(
-                    out=w2_w[:].rearrange("p (t m) -> p t m", t=PACK),
-                    in_=w2_raw[:].rearrange("p (m t) -> p t m", t=PACK),
-                )
-                for a in range(PASSES):
-                    round_weight(w3_bf[:, a * PACK * H : (a + 1) * PACK * H], w3_raw[a], nc.scalar.copy)
+        w3_bf = sbuf([P, PASSES * PACK * H], BF16, "w3_bf")
+        wgo_gain = [sbuf([P, S], F32, "wgo_gain%d" % t) for t in range(TILES)]
+        for t in range(1, TILES):
             for h in range(HALVES):
                 nc.vector.tensor_tensor(h_min[t][:, cols(h)], h_acc[t, h][:], lim_t[t][:, cols(h)], ALU.min)
-            fetch_first_half(lim_t[t][:, cols(0)], t - 1)
-            nc.vector.tensor_tensor(page[t][:].indirect(idx2[:]), h_min[t][:], wgs_t[t][:], ALU.mult)
+            fetch_x(lim_t[t][:, cols(0)], t - 1, 0)
+            turn_x(lim_t[t][:, cols(0)], x_bf0[:, t - 1, :], t - 1, 0)
+            nc.vector.tensor_tensor(page[t][:].indirect(idx2[:]), h_min[t][:], wgs_t[:], ALU.mult)
+        for t in range(TILES):
+            nc.scalar.activation(out=wgo_gain[t][:], in_=wgo_t[:], func=ACT.Copy, scale=gain_t[:, t : t + 1])
+        for a in range(PASSES):
+            round_weight(w3_bf[:, a * PACK * H : (a + 1) * PACK * H], w3_raw[a], nc.scalar.copy)
 
         y_acc = {}
 
         def second_sums(w3_q, x_q, h):
             codes, scales = x_q
-            for t in range(PACK):
-                acc = bank(t, h)
+            for t in range(TILES):
+                acc = bank([P, HALF], F32, t, h)
                 y_acc[t, h] = acc
                 table_first = (t, h) == (0, 0)
                 if table_first:
@@ -237,8 +252,8 @@ def tile_list_wheel_friction_page_kernel(
                     table_pass(acc, w3_q, 1, t, h, False, False)
                 nc.tensor.matmul_mx(
                     out=acc[:],
-                    lhsT=w2_w[:, t * P : (t + 1) * P].bitcast(FP4X4),
-                    lhsT_scale=w2_sc[:, t * P : (t + 1) * P],
+                    lhsT=w2_w[:, 2 * t * P : 2 * (t + 1) * P].bitcast(FP4X4),
+                    lhsT_scale=w2_sc[:, rows(t)],
                     rhs=codes[:].bitcast(FP8X4),
                     rhs_scale=scales[:],
                     start=not table_first,
@@ -248,45 +263,36 @@ def tile_list_wheel_friction_page_kernel(
                     table_pass(acc, w3_q, 0, t, h, False, False)
                     table_pass(acc, w3_q, 1, t, h, False, True)
 
-        y = {}
-
-        def finish_y(t, h, tag, bufs, magnitude):
-            y[t, h] = keep.tile([P, HALF], F32, name="y%d%d" % (t, h), tag=tag, bufs=bufs, align_bytes=64)
-            nc.scalar.activation(out=magnitude, in_=y_acc[t, h][:], func=ACT.Abs)
-            nc.scalar.activation(out=y[t, h][:], in_=magnitude, func=ACT.Copy, scale=gain_t[:, t : t + 1])
-
-        def put_y(t, h):
+        def put_y(t, h, tag=None):
+            magnitude = sbuf([P, HALF], F32, "magnitude%d%d" % (t, h), tag)
+            nc.scalar.activation(out=magnitude[:], in_=y_acc[t, h][:], func=ACT.Abs)
             nc.vector.tensor_tensor(
-                page[t][:].indirect(entries(idx4, h)), y[t, h][:], wgo_t[t // 2][:, t % 2, cols(h)], ALU.mult
+                page[t][:].indirect(entries(idx4, h)), magnitude[:], wgo_gain[t][:, cols(h)], ALU.mult
             )
 
-        x_planes = keep.tile([P, PACK * HALF], BF16, name="x_planes", align_bytes=64)
-        fetch_first_half(lim0[0][:], PACK - 1)
-        fetch(h_min[PACK - 1][:, cols(0)], 0, 1)
-        add_bias(x_planes[:, cols(0)], h_min[PACK - 1][:, cols(0)], 0)
-        w3_codes, w3_scales = quantise(w3_bf, "w3", tag="wgs3")
-        w3_q = [(w3_codes[:, a * H : (a + 1) * H], w3_scales[:, a * H : (a + 1) * H]) for a in range(PASSES)]
-        second_sums(w3_q, quantise(x_woven[0], "x_0"), 0)
-        fetch(h_min[PACK - 1][:, cols(1)], 1, 1)
-        add_bias(x_planes[:, cols(1)], h_min[PACK - 1][:, cols(1)], 1)
-        late = keep.tile([P, 2, HALF], F32, name="x_late", tag="x_woven0", align_bytes=64)
-        for t in (2, 3):
-            fetch(late[:, t - 2, :], t, 1)
-        finish_y(0, 0, "y00", 1, x_planes[:, 2 * HALF :].bitcast(F32))
-        for t in (2, 3):
-            add_bias(x_planes[:, cols(t)], late[:, t - 2, :], t)
-        finish_y(1, 0, "y10", 1, x_woven[1][:, : 2 * HALF].bitcast(F32))
+        last = TILES - 1
+        fetch_x(lim0[0][:], last, 0)
+        turn_x(lim0[0][:], x_bf0[:, last, :], last, 0)
+        woven0 = weave_x(0)
+        w3_all = quantise(w3_bf, "w3", tag="wgs_t")
+        w3_q = {(a, t): stationary(w3_all, a * H + t * P) for a in range(PASSES) for t in range(TILES)}
+        fetch_x(h_min[last][:, cols(0)], 0, 1)
+        fetch_x(h_min[last][:, cols(1)], 1, 1)
+        x_21 = sbuf([P, HALF], F32, "x_21", "w3_bf")
+        fetch_x(x_21[:], 2, 1)
+        second_sums(w3_q, quantise(woven0, "x_0"), 0)
+        x_31 = sbuf([P, HALF], F32, "x_31", "x_woven0")
+        fetch_x(x_31[:], last, 1)
         put_y(0, 0)
-        nc.scalar.copy(
-            out=x_woven[1][:].rearrange("p (c i) -> p c i", i=PACK),
-            in_=x_planes[:].rearrange("p (i c) -> p c i", i=PACK),
-        )
+        x_bf1 = sbuf([P, TILES, HALF], BF16, "x_bf1", "x_pairs0")
+        for t, buf in enumerate((h_min[last][:, cols(0)], h_min[last][:, cols(1)], x_21[:], x_31[:])):
+            turn_x(buf, x_bf1[:, t, :], t, 1)
         put_y(1, 0)
-        second_sums(w3_q, quantise(x_woven[1], "x_1", tag="y00"), 1)
-        for t in (2, 3):
-            finish_y(t, 0, "y_ring", 2, h_min[0][:, cols(t - 2)])
-            put_y(t, 0)
-        for t in range(PACK):
-            finish_y(t, 1, "y_ring", 2, h_min[1 + t // 2][:, cols(t % 2)])
+        woven1 = weave_x(1)
+        put_y(last, 0)
+        x_1 = quantise(woven1, "x_1")
+        put_y(2, 0, tag="x_pairs1")
+        second_sums(w3_q, x_1, 1)
+        for t in range(TILES):
             put_y(t, 1)
-            nc.sync.dma_start(out=out_rows[t], in_=page[t][:])
+            nc.sync.dma_start(out=out[rows(t), :], in_=page[t][:])

@@ -24,9 +24,11 @@ PASSES = K // K_PASS
 TILES = H // P
 HALF = 512
 HALVES = S // HALF
-BLOCKS = HALF // P
+QUARTER = HALF // 2
+PER_COLUMN = 16
 QUAD = 32
 SCALE_ROWS = 4
+RUN = 4
 
 
 def tile_list_wheel_friction_page_kernel(
@@ -46,7 +48,7 @@ def tile_list_wheel_friction_page_kernel(
             return slice(t * P, (t + 1) * P)
 
         def entries(list_tile, h):
-            return list_tile[:, h * HALF // 16 : (h + 1) * HALF // 16]
+            return list_tile[:, h * HALF // PER_COLUMN : (h + 1) * HALF // PER_COLUMN]
 
         def sbuf(shape, dtype, name, tag=None):
             return keep.tile(shape, dtype, name=name, tag=tag or name, align_bytes=64)
@@ -60,7 +62,7 @@ def tile_list_wheel_friction_page_kernel(
             return buf
 
         def load_list(src, name):
-            buf = lists.tile([P, S // 16], U16, name=name)
+            buf = lists.tile([P, S // PER_COLUMN], U16, name=name)
             nc.sync.dma_start(buf[:], src)
             return buf
 
@@ -74,12 +76,6 @@ def tile_list_wheel_friction_page_kernel(
 
         def load_weight(w, a, name):
             return load(w[a * K_PASS : (a + 1) * K_PASS].rearrange("(p i) c -> p i c", i=PACK), F32, name)
-
-        def load_per_row(vec, name):
-            buf = sbuf([P, TILES], F32, name)
-            with nc.allow_non_contiguous_dma(reason="one value for each row of the page"):
-                nc.sync.dma_start(out=buf[:], in_=vec.rearrange("(t p) -> p t", p=P))
-            return buf
 
         ident_bf = sbuf([P, P], BF16, "ident_bf")
         make_identity(nc, ident_bf[:])
@@ -117,8 +113,10 @@ def tile_list_wheel_friction_page_kernel(
         w1_late = [load_weight(w1[:, H // 2 :], a, "w1_late%d" % a) for a in range(PASSES)]
         idx3 = load_list(offs3, "idx3")
         load_tile_inputs(1)
-        bias_t = load_per_row(bias, "bias_t")
-        gain_t = load_per_row(gain, "gain_t")
+        vectors = sbuf([P, P], F32, "vectors")
+        nc.gpsimd.memset(vectors[:], 0.0)
+        for n, vec in enumerate((bias, gain)):
+            nc.sync.dma_start(out=vectors[n * TILES : (n + 1) * TILES, :], in_=vec.rearrange("(t p) -> t p", p=P))
         wgo_t = load(wgo, F32, "wgo_t")
         load_tile_inputs(2)
         w2_w = sbuf([P, 2 * H], U8, "w2_w")
@@ -126,8 +124,8 @@ def tile_list_wheel_friction_page_kernel(
 
         def round_weight(dst, raw, copy):
             copy(
-                out=dst.rearrange("p (c e i) -> p c i e", e=4, i=PACK),
-                in_=raw[:].rearrange("p i (c e) -> p c i e", e=4),
+                out=dst.rearrange("p (c e i) -> p c i e", e=RUN, i=PACK),
+                in_=raw[:].rearrange("p i (c e) -> p c i e", e=RUN),
             )
 
         def quantise(grouped, name, tag=None):
@@ -193,31 +191,38 @@ def tile_list_wheel_friction_page_kernel(
                 table_pass(h_acc[t, h], w1_q, 1 - first, t, h, False, True)
 
         h_min = [sbuf([P, S], F32, "h_min%d" % t) for t in range(TILES)]
-        x_pairs = [sbuf([P, BLOCKS, 2, P], F32, "x_pairs%d" % h) for h in range(HALVES)]
-
+        x_pairs = {(h, n): sbuf([P, 2, 2, P], F32, "x_pairs%d%d" % (h, n)) for h in range(HALVES) for n in range(2)}
         x_bf0 = sbuf([P, TILES, HALF], BF16, "x_bf0")
 
-        def fetch_x(buf, t, h):
-            nc.vector.tensor_copy(buf, page[t][:].indirect(entries(idx3, h)))
+        def fetch_x(buf, t, first, count):
+            offsets = idx3[:, first // PER_COLUMN : (first + count) // PER_COLUMN]
+            nc.vector.tensor_copy(buf, page[t][:].indirect(offsets))
 
-        def turn_x(buf, x_bf, t, h):
-            nc.scalar.activation(out=x_bf, in_=buf, func=ACT.Identity, bias=bias_t[:, t : t + 1])
-            turned = bank([P, BLOCKS, P], BF16, t % 2, 1)
-            for b in range(BLOCKS):
-                nc.tensor.transpose(turned[:, b, :], x_bf[:, rows(b)], ident_bf[:])
+        def turn_quarter(buf, x_bf, t, h, n):
+            part = slice(n * QUARTER, (n + 1) * QUARTER)
+            nc.scalar.activation(
+                out=x_bf[:, part], in_=buf[:, part], func=ACT.Identity, bias=per_row[:, t : t + 1]
+            )
+            turned = bank([P, 2, P], BF16, n, 1)
+            for b in range(2):
+                nc.tensor.transpose(turned[:, b, :], x_bf[:, rows(2 * n + b)], ident_bf[:])
             nc.scalar.copy(
-                out=x_pairs[h][:, :, :, t * QUAD : (t + 1) * QUAD],
+                out=x_pairs[h, n][:, :, :, t * QUAD : (t + 1) * QUAD],
                 in_=turned[:].bitcast(F32).rearrange("j b (q u) -> j b u q", u=2),
             )
 
+        def turn_x(buf, x_bf, t, h):
+            for n in range(2):
+                turn_quarter(buf, x_bf, t, h, n)
+
         def weave_x(h):
             woven = sbuf([P, PACK * HALF], BF16, "x_woven%d" % h)
-            words = woven[:].bitcast(F32).rearrange("p (b j u) -> p b j u", b=BLOCKS, u=2)
+            words = woven[:].bitcast(F32).rearrange("p (b j u) -> p b j u", j=P, u=2)
             for n in range(2):
                 back = bank([P, 2, 2, P], F32, 2 + n, 1)
                 for b in range(2):
                     for u in range(2):
-                        nc.tensor.transpose(back[:, b, u, :], x_pairs[h][:, 2 * n + b, u, :], ident_f32[:])
+                        nc.tensor.transpose(back[:, b, u, :], x_pairs[h, n][:, b, u, :], ident_f32[:])
                 nc.scalar.copy(out=words[:, 2 * n : 2 * n + 2], in_=back[:].rearrange("p b u j -> p b j u"))
             return woven
 
@@ -226,16 +231,22 @@ def tile_list_wheel_friction_page_kernel(
             nc.vector.tensor_tensor(
                 page[0][:].indirect(entries(idx2, h)), h_min[0][:, cols(h)], wgs_t[:, cols(h)], ALU.mult
             )
+        vectors_turned = bank([P, P], F32, 0, 0)
+        nc.tensor.transpose(vectors_turned[:], vectors[:], ident_f32[:])
+        per_row = sbuf([P, 2 * TILES], F32, "per_row")
+        nc.scalar.copy(out=per_row[:], in_=vectors_turned[:, : 2 * TILES])
         w3_bf = sbuf([P, PASSES * PACK * H], BF16, "w3_bf")
         wgo_gain = [sbuf([P, S], F32, "wgo_gain%d" % t) for t in range(TILES)]
         for t in range(1, TILES):
             for h in range(HALVES):
                 nc.vector.tensor_tensor(h_min[t][:, cols(h)], h_acc[t, h][:], lim_t[t][:, cols(h)], ALU.min)
-            fetch_x(lim_t[t][:, cols(0)], t - 1, 0)
+            fetch_x(lim_t[t][:, cols(0)], t - 1, 0, HALF)
             turn_x(lim_t[t][:, cols(0)], x_bf0[:, t - 1, :], t - 1, 0)
             nc.vector.tensor_tensor(page[t][:].indirect(idx2[:]), h_min[t][:], wgs_t[:], ALU.mult)
         for t in range(TILES):
-            nc.scalar.activation(out=wgo_gain[t][:], in_=wgo_t[:], func=ACT.Copy, scale=gain_t[:, t : t + 1])
+            nc.scalar.activation(
+                out=wgo_gain[t][:], in_=wgo_t[:], func=ACT.Copy, scale=per_row[:, TILES + t : TILES + t + 1]
+            )
         for a in range(PASSES):
             round_weight(w3_bf[:, a * PACK * H : (a + 1) * PACK * H], w3_raw[a], nc.scalar.copy)
 
@@ -271,27 +282,28 @@ def tile_list_wheel_friction_page_kernel(
             )
 
         last = TILES - 1
-        fetch_x(lim0[0][:], last, 0)
-        turn_x(lim0[0][:], x_bf0[:, last, :], last, 0)
+        for n in range(2):
+            fetch_x(lim0[0][:, n * QUARTER : (n + 1) * QUARTER], last, n * QUARTER, QUARTER)
+            turn_quarter(lim0[0][:], x_bf0[:, last, :], last, 0, n)
         woven0 = weave_x(0)
         w3_all = quantise(w3_bf, "w3", tag="wgs_t")
         w3_q = {(a, t): stationary(w3_all, a * H + t * P) for a in range(PASSES) for t in range(TILES)}
-        fetch_x(h_min[last][:, cols(0)], 0, 1)
-        fetch_x(h_min[last][:, cols(1)], 1, 1)
-        x_21 = sbuf([P, HALF], F32, "x_21", "w3_bf")
-        fetch_x(x_21[:], 2, 1)
+        fetch_x(h_min[last][:, cols(0)], 0, HALF, HALF)
+        fetch_x(h_min[last][:, cols(1)], 1, HALF, HALF)
         second_sums(w3_q, quantise(woven0, "x_0"), 0)
-        x_31 = sbuf([P, HALF], F32, "x_31", "x_woven0")
-        fetch_x(x_31[:], last, 1)
+        x_late = sbuf([P, 2, HALF], F32, "x_late", "x_woven0")
+        for t in (2, 3):
+            fetch_x(x_late[:, t - 2, :], t, HALF, HALF)
+
         put_y(0, 0)
-        x_bf1 = sbuf([P, TILES, HALF], BF16, "x_bf1", "x_pairs0")
-        for t, buf in enumerate((h_min[last][:, cols(0)], h_min[last][:, cols(1)], x_21[:], x_31[:])):
+        x_bf1 = sbuf([P, TILES, HALF], BF16, "x_bf1", "x_pairs01")
+        for t, buf in enumerate((h_min[last][:, cols(0)], h_min[last][:, cols(1)], x_late[:, 0, :], x_late[:, 1, :])):
             turn_x(buf, x_bf1[:, t, :], t, 1)
         put_y(1, 0)
         woven1 = weave_x(1)
         put_y(last, 0)
         x_1 = quantise(woven1, "x_1")
-        put_y(2, 0, tag="x_pairs1")
+        put_y(2, 0, tag="x_pairs11")
         second_sums(w3_q, x_1, 1)
         for t in range(TILES):
             put_y(t, 1)

from contextlib import ExitStack

import concourse.mybir as mybir
from concourse.masks import make_identity

K, H, T, S, T2 = 1024, 512, 4096, 1024, 2048
FLOPS = 2 * S * H * (K + H + K)

F32 = mybir.dt.float32
BF16 = mybir.dt.bfloat16
I32 = mybir.dt.int32
U32 = mybir.dt.uint32
U16 = mybir.dt.uint16
U8 = mybir.dt.uint8
FP8X4 = mybir.dt.float8_e4m3fn_x4
FP4X4 = mybir.dt.float4_e2m1fn_x4
ACT = mybir.ActivationFunctionType
ALU = mybir.AluOpType

P = 128
PACK = 4
K_PASS = P * PACK
PASSES = K // K_PASS
TILES = H // P
HALF = 512
HALVES = S // HALF
QUARTER = HALF // 2
PER_COLUMN = 16
QUAD = 32
SCALE_ROWS = 4
RUN = 4


def tile_list_wheel_friction_page_kernel(
    tc, tab_words, tab_scales, offs, offs2, offs3, offs4, w1, lim, page0, wgs, bias,
    w2_words, w2_scales, w3, gain, wgo, out,
):
    nc = tc.nc
    with ExitStack() as ctx:
        lists = ctx.enter_context(tc.tile_pool(name="lists", bufs=1))
        keep = ctx.enter_context(tc.tile_pool(name="keep", bufs=1))
        psum = ctx.enter_context(tc.psum_pool(name="psum", bufs=1))

        def cols(h):
            return slice(h * HALF, (h + 1) * HALF)

        def rows(t):
            return slice(t * P, (t + 1) * P)

        def entries(list_tile, h):
            return list_tile[:, h * HALF // PER_COLUMN : (h + 1) * HALF // PER_COLUMN]

        def sbuf(shape, dtype, name, tag=None):
            return keep.tile(shape, dtype, name=name, tag=tag or name, align_bytes=64)

        def bank(shape, dtype, t, h):
            return psum.tile(shape, dtype, name="bank%d%d" % (t, h))

        def load(src, dtype, name):
            buf = sbuf(list(src.shape), dtype, name)
            nc.sync.dma_start(out=buf[:], in_=src)
            return buf

        def load_list(src, name):
            buf = lists.tile([P, S // PER_COLUMN], U16, name=name)
            nc.sync.dma_start(buf[:], src)
            return buf

        def load_table(a):
            buf = sbuf([P, T], U32, "tab_w%d" % a)
            nc.sync.dma_start(
                out=buf[:].bitcast(I32),
                in_=tab_words[a].rearrange("p c i -> p (c i)").bitcast(I32),
            )
            return buf

        def load_weight(w, a, name):
            return load(w[a * K_PASS : (a + 1) * K_PASS].rearrange("(p i) c -> p i c", i=PACK), F32, name)

        ident_bf = sbuf([P, P], BF16, "ident_bf")
        make_identity(nc, ident_bf[:])
        ident_f32 = sbuf([P, P], F32, "ident_f32")
        make_identity(nc, ident_f32[:])

        tab_sc = sbuf([P, T], U8, "tab_sc")
        nc.vector.memset(tab_sc[:].bitcast(I32), 0)
        w2_sc = sbuf([P, H], U8, "w2_sc")
        nc.vector.memset(w2_sc[:].bitcast(I32), 0)
        for g in (0, 2, 1, 3):
            nc.sync.dma_start(
                out=tab_sc[g * QUAD : g * QUAD + SCALE_ROWS * PASSES, :].bitcast(I32),
                in_=tab_scales[:, SCALE_ROWS * g : SCALE_ROWS * (g + 1), :].bitcast(I32),
            )

        idx = load_list(offs, "idx")
        w1_early = [load_weight(w1[:, : H // 2], a, "w1_early%d" % a) for a in range(PASSES)]
        w2_sc_rows = load(w2_scales[0].bitcast(I32).rearrange("(g r) c -> r g c", r=SCALE_ROWS), I32, "w2_sc_rows")
        tab_w = [load_table(0)]
        idx2 = load_list(offs2, "idx2")
        tab_w.append(load_table(1))
        lim0 = [load(lim[rows(0), cols(0)], F32, "lim0_0")]
        wgs_t = sbuf([P, S], F32, "wgs_t")
        nc.sync.dma_start(out=wgs_t[:, cols(0)], in_=wgs[:, cols(0)])
        page = [load(page0[rows(0), :], F32, "page0")]
        lim0.append(load(lim[rows(0), cols(1)], F32, "lim0_1"))
        nc.sync.dma_start(out=wgs_t[:, cols(1)], in_=wgs[:, cols(1)])
        lim_t = {}

        def load_tile_inputs(t):
            lim_t[t] = load(lim[rows(t), :], F32, "lim%d" % t)
            page.append(load(page0[rows(t), :], F32, "page%d" % t))

        w1_late = [load_weight(w1[:, H // 2 :], a, "w1_late%d" % a) for a in range(PASSES)]
        idx3 = load_list(offs3, "idx3")
        load_tile_inputs(1)
        vectors = sbuf([P, P], F32, "vectors")
        nc.gpsimd.memset(vectors[:], 0.0)
        for n, vec in enumerate((bias, gain)):
            nc.sync.dma_start(out=vectors[n * TILES : (n + 1) * TILES, :], in_=vec.rearrange("(t p) -> t p", p=P))
        wgo_t = load(wgo, F32, "wgo_t")
        load_tile_inputs(2)
        w2_w = sbuf([P, 2 * H], U8, "w2_w")
        nc.sync.dma_start(out=w2_w[:].bitcast(I32), in_=w2_words[0].bitcast(I32))

        def round_weight(dst, raw, copy):
            copy(
                out=dst.rearrange("p (c e i) -> p c i e", e=RUN, i=PACK),
                in_=raw[:].rearrange("p i (c e) -> p c i e", e=RUN),
            )

        def quantise(grouped, name, tag=None):
            width = grouped.shape[1] // PACK
            codes = sbuf([P, width], U32, name + "_codes", tag)
            scales = sbuf([P, width], U8, name + "_scales")
            nc.vector.quantize_mx(out=codes[:].bitcast(FP8X4), scales=scales[:], in_=grouped[:])
            return codes, scales

        def stationary(quantised, first):
            codes, scales = quantised
            return codes[:, first : first + P], scales[:, first : first + P]

        w1_q = {}
        for a, copy in enumerate((nc.scalar.copy, nc.vector.tensor_copy)):
            w1_bf = sbuf([P, PACK * H // 2], BF16, "w1_bf%d" % a)
            round_weight(w1_bf[:], w1_early[a], copy)
            early = quantise(w1_bf, "w1_early%d" % a)
            for t in range(TILES // 2):
                w1_q[a, t] = stationary(early, t * P)

        for g in range(P // QUAD):
            nc.vector.tensor_copy(
                out=w2_sc[g * QUAD : g * QUAD + SCALE_ROWS, :].bitcast(I32), in_=w2_sc_rows[:, g, :]
            )
        v_sc = sbuf([P, S], U8, "v_sc", "w1_bf1")
        nc.vector.tensor_copy(v_sc[:], tab_sc[:].indirect(idx[:]))
        v_w = [sbuf([P, S], U32, "v_w%d" % a) for a in range(PASSES)]
        nc.vector.tensor_copy(v_w[0][:], tab_w[0][:].indirect(idx[:]))
        for h in range(HALVES):
            nc.vector.tensor_copy(v_w[1][:, cols(h)], tab_w[1][:].indirect(entries(idx, h)))

        w1_late_bf = sbuf([P, PASSES, PACK * H // 2], BF16, "w1_late_bf")
        for a in range(PASSES):
            round_weight(w1_late_bf[:, a, :], w1_late[a], nc.scalar.copy)
        late = quantise(w1_late_bf[:].rearrange("p a c -> p (a c)"), "w1_late")
        for a in range(PASSES):
            for t in range(TILES // 2):
                w1_q[a, TILES // 2 + t] = stationary(late, a * H // 2 + t * P)

        w3_raw = [load_weight(w3, a, "w3_raw%d" % a) for a in range(PASSES)]
        load_tile_inputs(3)
        idx4 = load_list(offs4, "idx4")

        def table_pass(acc, w_q, a, t, h, start, stop):
            codes, scales = w_q[a, t]
            nc.tensor.matmul_mx(
                out=acc[:],
                lhsT=codes.bitcast(FP8X4),
                lhsT_scale=scales,
                rhs=v_w[a][:, cols(h)].bitcast(FP8X4),
                rhs_scale=v_sc[SCALE_ROWS * a :, cols(h)],
                start=start,
                stop=stop,
            )

        h_acc = {}
        for t in range(TILES):
            for h in range(HALVES):
                h_acc[t, h] = bank([P, HALF], F32, t, h)
                first = 0 if t == 0 else 1
                table_pass(h_acc[t, h], w1_q, first, t, h, True, False)
                table_pass(h_acc[t, h], w1_q, 1 - first, t, h, False, True)

        h_min = [sbuf([P, S], F32, "h_min%d" % t) for t in range(TILES)]
        x_pairs = {(h, n): sbuf([P, 2, 2, P], F32, "x_pairs%d%d" % (h, n)) for h in range(HALVES) for n in range(2)}
        x_bf0 = sbuf([P, TILES, HALF], BF16, "x_bf0")

        def fetch_x(buf, t, first, count):
            offsets = idx3[:, first // PER_COLUMN : (first + count) // PER_COLUMN]
            nc.vector.tensor_copy(buf, page[t][:].indirect(offsets))

        def turn_quarter(buf, x_bf, t, h, n):
            part = slice(n * QUARTER, (n + 1) * QUARTER)
            nc.scalar.activation(
                out=x_bf[:, part], in_=buf[:, part], func=ACT.Identity, bias=per_row[:, t : t + 1]
            )
            turned = bank([P, 2, P], BF16, n, 1)
            for b in range(2):
                nc.tensor.transpose(turned[:, b, :], x_bf[:, rows(2 * n + b)], ident_bf[:])
            nc.scalar.copy(
                out=x_pairs[h, n][:, :, :, t * QUAD : (t + 1) * QUAD],
                in_=turned[:].bitcast(F32).rearrange("j b (q u) -> j b u q", u=2),
            )

        def turn_x(buf, x_bf, t, h):
            for n in range(2):
                turn_quarter(buf, x_bf, t, h, n)

        def weave_x(h):
            woven = sbuf([P, PACK * HALF], BF16, "x_woven%d" % h)
            words = woven[:].bitcast(F32).rearrange("p (b j u) -> p b j u", j=P, u=2)
            for n in range(2):
                back = bank([P, 2, 2, P], F32, 2 + n, 1)
                for b in range(2):
                    for u in range(2):
                        nc.tensor.transpose(back[:, b, u, :], x_pairs[h, n][:, b, u, :], ident_f32[:])
                nc.scalar.copy(out=words[:, 2 * n : 2 * n + 2], in_=back[:].rearrange("p b u j -> p b j u"))
            return woven

        for h in range(HALVES):
            nc.vector.tensor_tensor(h_min[0][:, cols(h)], h_acc[0, h][:], lim0[h][:], ALU.min)
            nc.vector.tensor_tensor(
                page[0][:].indirect(entries(idx2, h)), h_min[0][:, cols(h)], wgs_t[:, cols(h)], ALU.mult
            )
        vectors_turned = bank([P, P], F32, 0, 0)
        nc.tensor.transpose(vectors_turned[:], vectors[:], ident_f32[:])
        per_row = sbuf([P, 2 * TILES], F32, "per_row")
        nc.scalar.copy(out=per_row[:], in_=vectors_turned[:, : 2 * TILES])
        w3_bf = sbuf([P, PASSES * PACK * H], BF16, "w3_bf")
        wgo_gain = [sbuf([P, S], F32, "wgo_gain%d" % t) for t in range(TILES)]
        for t in range(1, TILES):
            for h in range(HALVES):
                nc.vector.tensor_tensor(h_min[t][:, cols(h)], h_acc[t, h][:], lim_t[t][:, cols(h)], ALU.min)
            fetch_x(lim_t[t][:, cols(0)], t - 1, 0, HALF)
            turn_x(lim_t[t][:, cols(0)], x_bf0[:, t - 1, :], t - 1, 0)
            nc.vector.tensor_tensor(page[t][:].indirect(idx2[:]), h_min[t][:], wgs_t[:], ALU.mult)
        for t in range(TILES):
            nc.scalar.activation(
                out=wgo_gain[t][:], in_=wgo_t[:], func=ACT.Copy, scale=per_row[:, TILES + t : TILES + t + 1]
            )
        for a in range(PASSES):
            round_weight(w3_bf[:, a * PACK * H : (a + 1) * PACK * H], w3_raw[a], nc.scalar.copy)

        y_acc = {}

        def second_sums(w3_q, x_q, h):
            codes, scales = x_q
            for t in range(TILES):
                acc = bank([P, HALF], F32, t, h)
                y_acc[t, h] = acc
                table_first = (t, h) == (0, 0)
                if table_first:
                    table_pass(acc, w3_q, 0, t, h, True, False)
                    table_pass(acc, w3_q, 1, t, h, False, False)
                nc.tensor.matmul_mx(
                    out=acc[:],
                    lhsT=w2_w[:, 2 * t * P : 2 * (t + 1) * P].bitcast(FP4X4),
                    lhsT_scale=w2_sc[:, rows(t)],
                    rhs=codes[:].bitcast(FP8X4),
                    rhs_scale=scales[:],
                    start=not table_first,
                    stop=table_first,
                )
                if not table_first:
                    table_pass(acc, w3_q, 0, t, h, False, False)
                    table_pass(acc, w3_q, 1, t, h, False, True)

        def put_y(t, h, tag=None):
            magnitude = sbuf([P, HALF], F32, "magnitude%d%d" % (t, h), tag)
            nc.scalar.activation(out=magnitude[:], in_=y_acc[t, h][:], func=ACT.Abs)
            nc.vector.tensor_tensor(
                page[t][:].indirect(entries(idx4, h)), magnitude[:], wgo_gain[t][:, cols(h)], ALU.mult
            )

        last = TILES - 1
        for n in range(2):
            fetch_x(lim0[0][:, n * QUARTER : (n + 1) * QUARTER], last, n * QUARTER, QUARTER)
            turn_quarter(lim0[0][:], x_bf0[:, last, :], last, 0, n)
        woven0 = weave_x(0)
        w3_all = quantise(w3_bf, "w3", tag="wgs_t")
        w3_q = {(a, t): stationary(w3_all, a * H + t * P) for a in range(PASSES) for t in range(TILES)}
        fetch_x(h_min[last][:, cols(0)], 0, HALF, HALF)
        fetch_x(h_min[last][:, cols(1)], 1, HALF, HALF)
        second_sums(w3_q, quantise(woven0, "x_0"), 0)
        x_late = sbuf([P, 2, HALF], F32, "x_late", "x_woven0")
        for t in (2, 3):
            fetch_x(x_late[:, t - 2, :], t, HALF, HALF)

        put_y(0, 0)
        x_bf1 = sbuf([P, TILES, HALF], BF16, "x_bf1", "x_pairs01")
        for t, buf in enumerate((h_min[last][:, cols(0)], h_min[last][:, cols(1)], x_late[:, 0, :], x_late[:, 1, :])):
            turn_x(buf, x_bf1[:, t, :], t, 1)
        put_y(1, 0)
        woven1 = weave_x(1)
        put_y(last, 0)
        x_1 = quantise(woven1, "x_1")
        put_y(2, 0, tag="x_pairs11")
        second_sums(w3_q, x_1, 1)
        for t in range(TILES):
            put_y(t, 1)
            nc.sync.dma_start(out=out[rows(t), :], in_=page[t][:])
